import numpy as np, ml_dtypes
CORES = [73,201,329,457,330]
N = 5
import mx_ref
NC, G = 128, 2
EPS = 0.001
BF = ml_dtypes.bfloat16
def cut(t, i, w=512):
    return t[:, w * i:w * i + w]
def tile(rs):
    return np.stack(rs, axis=2).reshape(128, -1).astype(BF)
def layer(w, X):
    out = []
    for i in range(G):
        for t in range(len(X)):
            p = mx_ref.matmul(mx_ref.quantize(cut(w, len(X) * i + t)), X[t])
            z = p if t == 0 else z + p
        out.append(z)
    return out
def setup_inputs(rng):
    def f(*shape):
        return mx_ref.flush((rng.standard_normal(shape, dtype=np.float32) * np.exp2(rng.integers(-2, 3, shape[:-1] + (1,)))).astype(BF))
    return {"x": f(N, 128, 4 * NC), "w1": f(N, 128, G * 512), "w2": f(N, 128, 512)}
def setup_inputs_blocks(rng):
    d = setup_inputs(rng)
    for k in ("x", "w1", "w2"): d[k] = mx_ref.spread(d[k], rng, 4)
    return d
def setup_inputs_wide(rng):
    d = setup_inputs(rng)
    for k in ("x", "w1", "w2"): d[k] = mx_ref.flush((d[k].astype(np.float32) * np.exp2(rng.integers(-6, 7, (N, 1, 1))).astype(np.float32)).astype(BF))
    return d
def setup_inputs_cols(rng):
    d = setup_inputs(rng); v = d["x"].astype(np.float32).reshape(N, 128, -1, 4)
    d["x"] = mx_ref.flush((v * np.exp2(rng.integers(-6, 7, (N, 1, v.shape[2], 1))).astype(np.float32)).reshape(d["x"].shape).astype(BF))
    return d
def setup_inputs_faint(rng):
    d = setup_inputs(rng); d["x"] = mx_ref.flush((d["x"].astype(np.float32) * np.float32(2.0 ** -12)).astype(BF))
    return d
def reference(x, w1, w2, own=None):
    h = np.zeros((N, 128, 4 * NC), BF)
    for r in range(N):
        Z = layer(w1[r], [mx_ref.quantize(x[r])]); R = [np.maximum(k * z, 0) for z in Z for k in (1, -1)]
        ms = sum((v.astype(np.float64) ** 2).sum(axis=0) for v in R) / 512
        s = (1 / np.sqrt(ms + EPS)).astype(np.float32)
        h[r] = tile([v * s for v in R])
    use = h if own is None else own["h"]
    H = [mx_ref.quantize(use[j]) for j in range(N)]
    y = np.zeros((N, 128, N * NC), np.float32)
    for r in range(N):
        qw = mx_ref.quantize(w2[r])
        for j in range(N):
            y[r][:, NC * j:NC * j + NC] = mx_ref.matmul(qw, H[j])
    return {"h": h, "y": y}

from concourse.bass import DstId, RemoteDMATransfer
from concourse.mybir import dt, AluOpType, ActivationFunctionType

N, NC, EPS = 5, 128, 0.001

SCRATCH = {
    "xb": ("sbuf", [128, 512], "bfloat16"),
    "w1b": ("sbuf", [128, 1024], "bfloat16"),
    "w2b": ("sbuf", [128, 512], "bfloat16"),
    "xq": ("sbuf", [128, 128], "float8_e4m3fn_x4"),
    "xs": ("sbuf", [128, 128], "uint8"),
    "w1q": ("sbuf", [128, 256], "float8_e4m3fn_x4"),
    "w1s": ("sbuf", [128, 256], "uint8"),
    "w2q": ("sbuf", [128, 128], "float8_e4m3fn_x4"),
    "w2s": ("sbuf", [128, 128], "uint8"),
    "hq": ("sbuf", [128, N * NC], "float8_e4m3fn_x4"),
    "hs": ("sbuf", [128, N * NC], "uint8"),
    "ones": ("sbuf", [128, 128], "bfloat16"),
    "ident": ("sbuf", [128, 128], "bfloat16"),
    "sq": ("sbuf", [128, 256], "float32"),
    "col": ("sbuf", [128, 24], "float32"),
    "pb": ("sbuf", [128, 256], "bfloat16"),
    "ht": ("sbuf", [128, 512], "bfloat16"),
    "yb": ("sbuf", [128, N * NC], "float32"),
    "ps": ("psum", [128, 512 * 8], "float32"),
}
SEMAPHORES = (["lx", "lw1", "lw2", "ones", "ident", "qx", "qa", "qb", "qw2", "z0", "z1", "ss0", "ss1", "b0", "aa", "inv", "rr",
               "p0", "p1", "t0", "t1", "e0", "e1", "e2", "e3", "qh", "sth", "sent"]
              + [n + str(k) for n in ("c", "s", "y", "v", "st") for k in range(N)])


def _plan(cores, topo):
    R = range(len(cores))
    place = lambda r: (topo.host(cores[r]), topo.chip(cores[r]))
    rack = lambda r: topo.rack(topo.host(cores[r]))
    can = lambda a, b: topo.may_write(cores[a], cores[b])
    slot = {r: k for k, r in enumerate(sorted(R, key=lambda r: cores[r]))}
    gates, home, fwd, turns = {}, {}, {r: {} for r in R}, {}
    for i in R:
        by_chip = {}
        for j in R:
            if j != i and can(i, j):
                by_chip.setdefault(place(j), []).append(j)
        home[i] = by_chip.pop(place(i), [])
        gates[i] = []
        for ch, members in by_chip.items():
            k = turns.get(ch, 0)
            turns[ch] = k + 1
            gate = members[k % len(members)]
            gates[i].append(gate)
            for m in members:
                if m != gate:
                    fwd[gate].setdefault(i, []).append(m)
        for j in R:
            if j != i and not can(i, j):
                k = [x for x in gates[i] if can(x, j) and rack(x) == rack(j)][0]
                fwd[k].setdefault(i, []).append(j)
    split = lambda r, ds: ([d for d in ds if place(d) != place(r)], [d for d in ds if place(d) == place(r)])
    steps, when = {r: [] for r in R}, {r: {r: 0.0} for r in R}
    for i in R:
        far_duty = lambda x: 0 if split(x, fwd[x].get(i, []))[0] else 1
        order = sorted(gates[i], key=far_duty)
        for n, x in enumerate(order):
            steps[i].append(([i], [x], home[i] if n == len(order) - 1 else []))
            when[x][i] = n + 2.5
        for x in home[i]:
            when[x][i] = 1.0
    for k in R:
        todo = sorted(fwd[k].items(), key=lambda e: (when[k][e[0]], slot[e[0]]))
        merged = []
        for tile, ds in todo:
            if merged and merged[-1][1] == ds and slot[tile] == slot[merged[-1][0][-1]] + 1:
                merged[-1][0].append(tile)
            else:
                merged.append(([tile], ds))
        busy = 0.0
        for tiles, ds in merged:
            off, on = split(k, ds)
            steps[k].append((tiles, off, on))
            busy = max(busy, max(when[k][t] for t in tiles))
            for d in on:
                for t in tiles:
                    when[d][t] = busy + 1.0
            for d in off:
                busy += 1.0
                for t in tiles:
                    when[d][t] = busy + 1.5
    return slot, steps, when


def rank_program(g, core, T, topo):
    rank = T.rank_of(core)
    if rank is None:
        return
    S, A, F = T.sem, AluOpType, ActivationFunctionType
    v, s, t, q = g.vector, g.scalar, g.tensor, g.sync
    cores = T.cores
    slot, steps, when = _plan(cores, topo)
    bank = lambda b, n=NC: T.ps[:, 512 * b:512 * b + n]
    col = lambda k: T.col[:, 4 * k:4 * k + 1]
    SS0, SS1, B0, AA, RR, INV = range(6)
    bits = lambda m: bin(m).count("1")

    def masks(src, off, on):
        c = cores[src]
        away = 0
        for d in cores:
            if (topo.host(d), topo.chip(d)) != (topo.host(c), topo.chip(c)) and topo.may_write(c, d):
                away |= topo.mask(c, d)
        m_off = away
        for d in off:
            m_off &= topo.mask(c, cores[d])
        m_on = ~away
        for d in on:
            m_on &= topo.mask(c, cores[d])
        return m_off, m_on

    landed = {}
    for src in range(N):
        for tiles, off, on in steps[src]:
            m_off, m_on = masks(src, off, on)
            for ds, m in ((off, m_off), (on, m_on)):
                if rank in ds:
                    for tl in tiles:
                        landed[tl] = (tiles[0], bits(m))

    q.dma_start(T.xb[:], T.x[:]).then_inc(S.lx, 16)
    s.dma_start(T.w1b[:], T.w1[:]).then_inc(S.lw1, 16)
    q.dma_start(T.w2b[:], T.w2[:]).then_inc(S.lw2, 16)

    v.memset(T.ones[:], 1.0).then_inc(S.ones, 1)
    g.wait_ge(S.ones, 1)
    g.affine_select(T.ident[:], T.ones[:], [[-1, 128]], A.is_equal, 0.0, 0, 1).then_inc(S.ident, 1)

    v.wait_ge(S.lx, 16)
    v.quantize_mx(T.xq[:], T.xs[:], T.xb[:]).then_inc(S.qx, 1)
    v.wait_ge(S.lw1, 16)
    v.quantize_mx(T.w1q[:, 0:128], T.w1s[:, 0:128], T.w1b[:, 0:512]).then_inc(S.qa, 1)
    v.quantize_mx(T.w1q[:, 128:256], T.w1s[:, 128:256], T.w1b[:, 512:1024]).then_inc(S.qb, 1)
    t.wait_ge(S.qx, 1)
    t.wait_ge(S.qa, 1)
    t.matmul_mx(bank(0), T.xq[:], T.xs[:], T.w1q[:, 0:128], T.w1s[:, 0:128], True, True).then_inc(S.z0, 1)
    t.wait_ge(S.qb, 1)
    t.matmul_mx(bank(1), T.xq[:], T.xs[:], T.w1q[:, 128:256], T.w1s[:, 128:256], True, True).then_inc(S.z1, 1)

    s.wait_ge(S.z0, 1)
    s.activation(T.sq[:, 0:128], bank(0), F.Square, accum_out=col(SS0)).then_inc(S.ss0, 1)
    s.wait_ge(S.z1, 1)
    s.activation(T.sq[:, 128:256], bank(1), F.Square, accum_out=col(SS1)).then_inc(S.ss1, 1)
    v.wait_ge(S.ss0, 1)
    v.tensor_scalar(col(B0), col(SS0), 1.0 / 512, EPS, A.mult, A.add).then_inc(S.b0, 1)
    s.wait_ge(S.ss1, 1)
    s.wait_ge(S.b0, 1)
    s.activation(col(RR), col(SS1), F.Sqrt, bias=col(B0), scale=1.0 / 512).then_inc(S.rr, 1)
    v.wait_ge(S.ss1, 1)
    v.wait_ge(S.b0, 1)
    v.tensor_scalar(col(AA), col(SS1), 1.0 / 512, col(B0), A.mult, A.add).then_inc(S.aa, 1)
    v.wait_ge(S.aa, 1)
    v.reciprocal(col(INV), col(AA)).then_inc(S.inv, 1)

    v.wait_ge(S.inv, 1)
    v.wait_ge(S.rr, 1)
    v.tensor_scalar(T.pb[:, 0:128], bank(0), col(INV), col(RR), A.mult, A.mult).then_inc(S.p0, 1)
    v.tensor_scalar(T.pb[:, 128:256], bank(1), col(INV), col(RR), A.mult, A.mult).then_inc(S.p1, 1)
    t.wait_ge(S.ident, 1)
    t.wait_ge(S.p0, 1)
    t.matmul(bank(2), T.pb[:, 0:128], T.ident[:], True, True).then_inc(S.t0, 1)
    t.wait_ge(S.p1, 1)
    t.matmul(bank(3), T.pb[:, 128:256], T.ident[:], True, True).then_inc(S.t1, 1)
    v.wait_ge(S.t0, 1)
    v.tensor_scalar(T.ht[:, 0:512:4], bank(2), 0.0, None, A.max).then_inc(S.e0, 1)
    v.tensor_scalar(T.ht[:, 1:512:4], bank(2), -1.0, 0.0, A.mult, A.max).then_inc(S.e1, 1)
    s.wait_ge(S.t1, 1)
    s.activation(T.ht[:, 2:512:4], bank(3), F.Relu).then_inc(S.e2, 1)
    s.activation(T.ht[:, 3:512:4], bank(3), F.Relu, scale=-1.0).then_inc(S.e3, 1)

    own = slice(NC * slot[rank], NC * slot[rank] + NC)
    for e in (S.e0, S.e1, S.e2, S.e3):
        v.wait_ge(e, 1)
        q.wait_ge(e, 1)
    v.quantize_mx(T.hq[:, own], T.hs[:, own], T.ht[:]).then_inc(S.qh, 1)
    q.dma_start(T.h[:], T.ht[:]).then_inc(S.sth, 16)
    v.wait_ge(S.lw2, 16)
    v.quantize_mx(T.w2q[:], T.w2s[:], T.w2b[:]).then_inc(S.qw2, 1)

    sent = 0
    g.wait_ge(S.qh, 1)
    for tiles, off, on in steps[rank]:
        lo, hi = NC * slot[tiles[0]], NC * slot[tiles[-1]] + NC
        m_off, m_on = masks(rank, off, on)
        for kind in ("c", "s"):
            view = (lambda: T.hq[:, lo:hi].bitcast(dt.uint8)) if kind == "c" else (lambda: T.hs[:, lo:hi])
            for tl in tiles:
                if tl != rank:
                    g.wait_ge(S[kind + str(landed[tl][0])], landed[tl][1])
            transfers = []
            for ds, m in ((off, m_off), (on, m_on)):
                if ds:
                    ids = []
                    for d in ds:
                        rid, pid = topo.addr(cores[d], core)
                        ids.append(DstId(rid=rid, pnc=pid))
                    transfers.append(RemoteDMATransfer(dst_ids=ids, dma_engine_mask=m, remote_sem=S[kind + str(tiles[0])],
                                                       srcs=[view()], dsts=[view() for _ in ds]))
                    sent += bits(m)
            g.remote_dma_fused(transfers, local_sem=S.sent)

    order = sorted(range(N), key=lambda j: when[rank][j])
    for k, j in enumerate(order):
        b = (4, 5, 6, 7, 0)[k]
        if j == rank:
            t.wait_ge(S.qh, 1)
            t.wait_ge(S.qw2, 1)
        else:
            t.wait_ge(S["c" + str(landed[j][0])], landed[j][1])
            t.wait_ge(S["s" + str(landed[j][0])], landed[j][1])
        if b == 0:
            t.wait_ge(S.ss0, 1)
        cs = slice(NC * slot[j], NC * slot[j] + NC)
        t.matmul_mx(bank(b), T.w2q[:], T.w2s[:], T.hq[:, cs], T.hs[:, cs], True, True).then_inc(S["y" + str(k)], 1)
        blk = slice(NC * j, NC * j + NC)
        if k % 2 == 0:
            v.wait_ge(S["y" + str(k)], 1)
            v.tensor_copy(T.yb[:, blk], bank(b)).then_inc(S["v" + str(k)], 1)
            q.wait_ge(S["v" + str(k)], 1)
            q.dma_start(T.y[:, blk], T.yb[:, blk]).then_inc(S["st" + str(k)], 16)
        else:
            s.wait_ge(S["y" + str(k)], 1)
            s.activation(T.yb[:, blk], bank(b), F.Copy).then_inc(S["v" + str(k)], 1)
            s.wait_ge(S["v" + str(k)], 1)
            s.dma_start(T.y[:, blk], T.yb[:, blk]).then_inc(S["st" + str(k)], 16)

    g.wait_ge(S.sent, sent)
    g.wait_ge(S.sth, 16)
    for k in range(N):
        g.wait_ge(S["st" + str(k)], 16)
